import numpy as np, ml_dtypes
CORES = [1,129,9,137,57,185,105,233,113,241,121,249]
N = 12
KB, QP = 1, 256
MEM = [0,11]
WID = [256,128,32,160,224,32,160,128,160,192,224,96]
def setup_inputs(rng):
    return {"q": rng.standard_normal((N, 128, QP), dtype=np.float32).astype(ml_dtypes.bfloat16), "k": rng.standard_normal((N, 128, KB * 128), dtype=np.float32).astype(ml_dtypes.bfloat16), "v": rng.standard_normal((N, 128, KB * 128), dtype=np.float32).astype(ml_dtypes.bfloat16)}
def setup_inputs_big(rng):
    d = setup_inputs(rng)
    for k in ("q", "k", "v"): d[k] = (d[k].astype(np.float32) * 1024.0).astype(d[k].dtype)
    return d
def setup_inputs_small(rng):
    d = setup_inputs(rng)
    for k in ("q", "k", "v"): d[k] = (d[k].astype(np.float32) * (1 / 1024.0)).astype(d[k].dtype)
    return d
def setup_inputs_apart(rng):
    d = setup_inputs(rng)
    f = (10.0 ** rng.permutation(np.linspace(-1.5, 1.5, N))).astype(np.float32).reshape(N, 1, 1)
    for k in ("q", "k", "v"): d[k] = (d[k].astype(np.float32) * f).astype(d[k].dtype)
    return d
def whole(q, k, v):
    Q, K, V = q.astype(np.float64), k.astype(np.float64), v.astype(np.float64)
    y = np.zeros((N, 128, QP))
    for r in range(N):
        for j in MEM:
            for b in range(KB):
                S = np.maximum(K[j][:, 128 * b:128 * b + 128].T @ Q[r], 0.0)
                y[r] += V[j][:, 128 * b:128 * b + 128].T @ S
    return {"y": y.astype(ml_dtypes.bfloat16 if q.dtype != np.float64 else np.float64)}
def reference(q, k, v):
    o = whole(q, k, v)["y"].copy()
    for r in range(N):
        o[r][:, WID[r]:] = np.nan
    return {"y": o}

@@ -1,0 +1,118 @@
+from concourse.bass import DstId, RemoteDMATransfer
+from concourse.mybir import AluOpType
+
+ND = 4
+
+SCRATCH = {
+    "kvd": ("dram", [128, 256], "bfloat16"),
+    "kv0": ("sbuf", [128, 256], "bfloat16"),
+    "kv1": ("sbuf", [128, 256], "bfloat16"),
+    "qs": ("sbuf", [128, 256], "bfloat16"),
+    "zs": ("sbuf", [128, 256], "float32"),
+    "s0": ("sbuf", [128, 256], "bfloat16"),
+    "s1": ("sbuf", [128, 256], "bfloat16"),
+    "ys": ("sbuf", [128, 256], "bfloat16"),
+    "p0": ("psum", [128, 512], "float32"),
+    "p1": ("psum", [128, 512], "float32"),
+    "po": ("psum", [128, 512], "float32"),
+}
+SEMAPHORES = ["ld", "lq", "got", "sent", "a0", "a1", "zf", "m0", "m1", "r0", "r1", "mo", "cp", "st"]
+
+
+def _count(mask):
+    return bin(mask).count("1")
+
+
+def _plan(T, topo):
+    cores, wid = list(T.cores), T.tables["WID"]
+    world = range(topo.CORES_PER_HOST * (1 + max(topo.host(c) for c in cores)))
+    trees = []
+    for m in T.tables["MEM"]:
+        s = cores[m]
+        dests = sorted((c for c in cores if c != s), key=lambda c: -wid[T.rank_of(c)])
+        helpers = [c for c in world
+                   if (topo.host(c), topo.chip(c)) == (topo.host(s), topo.chip(s)) and T.rank_of(c) is None
+                   and all(topo.may_write(c, d) for d in dests)]
+        helpers.sort(key=lambda c: topo.die(c) != topo.die(s))
+        direct = [d for d in dests if topo.may_write(s, d)][:ND]
+        rest = [d for d in dests if d not in direct]
+        share = {h: rest[i::len(helpers)] for i, h in enumerate(helpers)}
+        trees.append((s, direct, helpers, share))
+    return trees
+
+
+def _send(g, T, topo, core, dests, out_name, sem, mask):
+    ids = []
+    for d in dests:
+        rid, pid = topo.addr(d, core)
+        ids.append(DstId(rid=rid, pnc=pid))
+    g.remote_dma_fused([RemoteDMATransfer(dst_ids=ids, dma_engine_mask=mask, remote_sem=sem, srcs=[T.kvd[:, :]],
+                                          dsts=[T[out_name][:, :] for _ in dests], alu_op=0)], local_sem=T.sem.sent)
+    return _count(mask)
+
+
+def _common(topo, core, dests):
+    mask = topo.mask(core, dests[0])
+    for d in dests:
+        mask &= topo.mask(core, d)
+    return mask
+
+
+def rank_program(g, core, T, topo):
+    trees = _plan(T, topo)
+    rank = T.rank_of(core)
+    sent = 0
+
+    mine = [j for j, t in enumerate(trees) if t[0] == core]
+    for j in mine:
+        g.sync.dma_start(T.kvd[:, 0:128], T.k[:, :]).then_inc(T.sem.ld, 16)
+        g.scalar.dma_start(T.kvd[:, 128:256], T.v[:, :]).then_inc(T.sem.ld, 16)
+
+    if rank is not None:
+        W = T.tables["WID"][rank]
+        g.sync.dma_start(T.qs[:, 0:W], T.q[:, 0:W]).then_inc(T.sem.lq, 16)
+        g.vector.memset(T.zs[:, 0:W], 0.0).then_inc(T.sem.zf, 1)
+        for j in mine:
+            g.sync.dma_start(T["kv%d" % j][:, 0:128], T.k[:, :]).then_inc(T.sem["a%d" % j], 16)
+            g.scalar.dma_start(T["kv%d" % j][:, 128:256], T.v[:, :]).then_inc(T.sem["a%d" % j], 16)
+
+    need, late = {}, {}
+    for j, (s, direct, helpers, share) in enumerate(trees):
+        off = _common(topo, s, direct)
+        on = _common(topo, s, helpers) & ~off
+        if core == s:
+            need[j], late[j] = 32, (0, 0)
+            g.wait_ge(T.sem.ld, 32)
+            sent += _send(g, T, topo, core, helpers, "kvd", T.sem.got, on)
+            sent += _send(g, T, topo, core, direct, "kv%d" % j, T.sem["a%d" % j], off)
+        elif core in share:
+            g.wait_ge(T.sem.got, _count(on))
+            sent += _send(g, T, topo, core, share[core], "kv%d" % j, T.sem["a%d" % j], _common(topo, core, share[core]))
+        elif core in direct:
+            need[j], late[j] = _count(off), (1, direct.index(core))
+        elif rank is not None:
+            h = [x for x in helpers if core in share[x]][0]
+            need[j], late[j] = _count(_common(topo, h, share[h])), (2, share[h].index(core), not topo.may_write(s, core))
+    if sent:
+        g.wait_ge(T.sem.sent, sent)
+    if rank is None:
+        return
+
+    order = sorted(need, key=lambda j: late[j])
+    te, ve = g.tensor, g.vector
+    te.wait_ge(T.sem.lq, 16)
+    ve.wait_ge(T.sem.zf, 1)
+    for j in order:
+        te.wait_ge(T.sem["a%d" % j], need[j])
+        te.matmul(T["p%d" % j][:, 0:W], T["kv%d" % j][:, 0:128], T.qs[:, 0:W], start=True, stop=True).then_inc(T.sem["m%d" % j], 1)
+        ve.wait_ge(T.sem["m%d" % j], 1)
+        ve.tensor_tensor(T["s%d" % j][:, 0:W], T["p%d" % j][:, 0:W], T.zs[:, 0:W], AluOpType.max).then_inc(T.sem["r%d" % j], 1)
+    for i, j in enumerate(order):
+        te.wait_ge(T.sem["r%d" % j], 1)
+        mm = te.matmul(T.po[:, 0:W], T["kv%d" % j][:, 128:256], T["s%d" % j][:, 0:W], start=(i == 0), stop=(i == len(order) - 1))
+    mm.then_inc(T.sem.mo, 1)
+    ve.wait_ge(T.sem.mo, 1)
+    ve.tensor_copy(T.ys[:, 0:W], T.po[:, 0:W]).then_inc(T.sem.cp, 1)
+    g.sync.wait_ge(T.sem.cp, 1)
+    g.sync.dma_start(T.y[:, 0:W], T.ys[:, 0:W]).then_inc(T.sem.st, 16)
+    g.wait_ge(T.sem.st, 16)

@@ -1,12 +1,18 @@
 from concourse.bass import DstId, RemoteDMATransfer
 from concourse.mybir import AluOpType
 
-ND = 4
+ND = 3
+NH = 6
 
 SCRATCH = {
-    "kvd": ("dram", [128, 256], "bfloat16"),
-    "kv0": ("sbuf", [128, 256], "bfloat16"),
-    "kv1": ("sbuf", [128, 256], "bfloat16"),
+    "kd": ("dram", [128, 128], "bfloat16"),
+    "vd": ("dram", [128, 128], "bfloat16"),
+    "w0": ("dram", [128, 128], "bfloat16"),
+    "w1": ("dram", [128, 128], "bfloat16"),
+    "k0": ("sbuf", [128, 128], "bfloat16"),
+    "k1": ("sbuf", [128, 128], "bfloat16"),
+    "v0": ("sbuf", [128, 128], "bfloat16"),
+    "v1": ("sbuf", [128, 128], "bfloat16"),
     "qs": ("sbuf", [128, 256], "bfloat16"),
     "zs": ("sbuf", [128, 256], "float32"),
     "s0": ("sbuf", [128, 256], "bfloat16"),
@@ -16,7 +22,8 @@ SCRATCH = {
     "p1": ("psum", [128, 512], "float32"),
     "po": ("psum", [128, 512], "float32"),
 }
-SEMAPHORES = ["ld", "lq", "got", "sent", "a0", "a1", "zf", "m0", "m1", "r0", "r1", "mo", "cp", "st"]
+SEMAPHORES = ["ldv", "ldk", "lq", "gv", "gk", "sent", "av0", "av1", "ak0", "ak1", "lv0", "lv1",
+              "zf", "m0", "m1", "r0", "r1", "mo", "cp", "st"]
 
 
 def _count(mask):
@@ -30,23 +37,34 @@ def _plan(T, topo):
     for m in T.tables["MEM"]:
         s = cores[m]
         dests = sorted((c for c in cores if c != s), key=lambda c: -wid[T.rank_of(c)])
-        helpers = [c for c in world
-                   if (topo.host(c), topo.chip(c)) == (topo.host(s), topo.chip(s)) and T.rank_of(c) is None
-                   and all(topo.may_write(c, d) for d in dests)]
-        helpers.sort(key=lambda c: topo.die(c) != topo.die(s))
         direct = [d for d in dests if topo.may_write(s, d)][:ND]
-        rest = [d for d in dests if d not in direct]
-        share = {h: rest[i::len(helpers)] for i, h in enumerate(helpers)}
-        trees.append((s, direct, helpers, share))
+        todo = [d for d in dests if d not in direct]
+        far = [d for d in todo if not topo.may_write(s, d)]
+        free = [c for c in world
+                if (topo.host(c), topo.chip(c)) == (topo.host(s), topo.chip(s)) and T.rank_of(c) is None]
+        owners = [c for c in free if all(topo.may_write(c, d) for d in dests)]
+        free = [c for c in free if c in owners or len(far) < len(todo)]
+        free.sort(key=lambda c: (c not in owners, topo.die(c) != topo.die(s)))
+        free = sorted(free[:NH], key=lambda c: (topo.die(c) != topo.die(s), c not in owners))
+        share = {h: [] for h in free}
+        while todo:
+            for h in free:
+                can = [d for d in todo if topo.may_write(h, d)]
+                can = [d for d in can if d in far] or can
+                if can:
+                    share[h].append(can[0])
+                    todo.remove(can[0])
+        helpers = [h for h in free if share[h]]
+        trees.append((s, direct, helpers, {h: share[h] for h in helpers}))
     return trees
 
 
-def _send(g, T, topo, core, dests, out_name, sem, mask):
+def _send(g, T, topo, core, dests, src, out_name, sem, mask):
     ids = []
     for d in dests:
         rid, pid = topo.addr(d, core)
         ids.append(DstId(rid=rid, pnc=pid))
-    g.remote_dma_fused([RemoteDMATransfer(dst_ids=ids, dma_engine_mask=mask, remote_sem=sem, srcs=[T.kvd[:, :]],
+    g.remote_dma_fused([RemoteDMATransfer(dst_ids=ids, dma_engine_mask=mask, remote_sem=sem, srcs=[T[src][:, :]],
                                           dsts=[T[out_name][:, :] for _ in dests], alu_op=0)], local_sem=T.sem.sent)
     return _count(mask)
 
@@ -65,51 +83,65 @@ def rank_program(g, core, T, topo):
 
     mine = [j for j, t in enumerate(trees) if t[0] == core]
     for j in mine:
-        g.sync.dma_start(T.kvd[:, 0:128], T.k[:, :]).then_inc(T.sem.ld, 16)
-        g.scalar.dma_start(T.kvd[:, 128:256], T.v[:, :]).then_inc(T.sem.ld, 16)
+        g.sync.dma_start(T.vd[:, :], T.v[:, :]).then_inc(T.sem.ldv, 16)
+        g.scalar.dma_start(T.kd[:, :], T.k[:, :]).then_inc(T.sem.ldk, 16)
 
     if rank is not None:
         W = T.tables["WID"][rank]
         g.sync.dma_start(T.qs[:, 0:W], T.q[:, 0:W]).then_inc(T.sem.lq, 16)
         g.vector.memset(T.zs[:, 0:W], 0.0).then_inc(T.sem.zf, 1)
         for j in mine:
-            g.sync.dma_start(T["kv%d" % j][:, 0:128], T.k[:, :]).then_inc(T.sem["a%d" % j], 16)
-            g.scalar.dma_start(T["kv%d" % j][:, 128:256], T.v[:, :]).then_inc(T.sem["a%d" % j], 16)
+            g.scalar.dma_start(T["k%d" % j][:, :], T.k[:, :]).then_inc(T.sem["ak%d" % j], 16)
+            g.sync.dma_start(T["v%d" % j][:, :], T.v[:, :]).then_inc(T.sem["lv%d" % j], 16)
 
     need, late = {}, {}
     for j, (s, direct, helpers, share) in enumerate(trees):
         off = _common(topo, s, direct)
         on = _common(topo, s, helpers) & ~off
+        w, kj, av, ak = "w%d" % j, "k%d" % j, T.sem["av%d" % j], T.sem["ak%d" % j]
         if core == s:
-            need[j], late[j] = 32, (0, 0)
-            g.wait_ge(T.sem.ld, 32)
-            sent += _send(g, T, topo, core, helpers, "kvd", T.sem.got, on)
-            sent += _send(g, T, topo, core, direct, "kv%d" % j, T.sem["a%d" % j], off)
+            need[j], late[j] = 16, (0, 0, 0)
+            g.wait_ge(T.sem.ldv, 16)
+            sent += _send(g, T, topo, core, helpers, "vd", "vd", T.sem.gv, on)
+            g.wait_ge(T.sem.ldk, 16)
+            sent += _send(g, T, topo, core, helpers, "kd", "kd", T.sem.gk, on)
+            sent += _send(g, T, topo, core, direct, "vd", w, av, off)
+            sent += _send(g, T, topo, core, direct, "kd", kj, ak, off)
         elif core in share:
-            g.wait_ge(T.sem.got, _count(on))
-            sent += _send(g, T, topo, core, share[core], "kv%d" % j, T.sem["a%d" % j], _common(topo, core, share[core]))
+            mask = _common(topo, core, share[core])
+            g.wait_ge(T.sem.gv, _count(on))
+            sent += _send(g, T, topo, core, share[core], "vd", w, av, mask)
+            g.wait_ge(T.sem.gk, _count(on))
+            sent += _send(g, T, topo, core, share[core], "kd", kj, ak, mask)
         elif core in direct:
-            need[j], late[j] = _count(off), (1, direct.index(core))
+            need[j], late[j] = _count(off), (1, direct.index(core), 0)
         elif rank is not None:
             h = [x for x in helpers if core in share[x]][0]
-            need[j], late[j] = _count(_common(topo, h, share[h])), (2, share[h].index(core), not topo.may_write(s, core))
+            need[j], late[j] = _count(_common(topo, h, share[h])), (2, share[h].index(core), helpers.index(h))
     if sent:
         g.wait_ge(T.sem.sent, sent)
     if rank is None:
         return
+
+    for j in need:
+        if j not in mine:
+            qu = g.scalar if j % 2 else g.sync
+            qu.wait_ge(T.sem["av%d" % j], need[j])
+            qu.dma_start(T["v%d" % j][:, :], T["w%d" % j][:, :]).then_inc(T.sem["lv%d" % j], 16)
 
     order = sorted(need, key=lambda j: late[j])
     te, ve = g.tensor, g.vector
     te.wait_ge(T.sem.lq, 16)
     ve.wait_ge(T.sem.zf, 1)
     for j in order:
-        te.wait_ge(T.sem["a%d" % j], need[j])
-        te.matmul(T["p%d" % j][:, 0:W], T["kv%d" % j][:, 0:128], T.qs[:, 0:W], start=True, stop=True).then_inc(T.sem["m%d" % j], 1)
+        te.wait_ge(T.sem["ak%d" % j], need[j])
+        te.matmul(T["p%d" % j][:, 0:W], T["k%d" % j][:, :], T.qs[:, 0:W], start=True, stop=True).then_inc(T.sem["m%d" % j], 1)
         ve.wait_ge(T.sem["m%d" % j], 1)
         ve.tensor_tensor(T["s%d" % j][:, 0:W], T["p%d" % j][:, 0:W], T.zs[:, 0:W], AluOpType.max).then_inc(T.sem["r%d" % j], 1)
     for i, j in enumerate(order):
         te.wait_ge(T.sem["r%d" % j], 1)
-        mm = te.matmul(T.po[:, 0:W], T["kv%d" % j][:, 128:256], T["s%d" % j][:, 0:W], start=(i == 0), stop=(i == len(order) - 1))
+        te.wait_ge(T.sem["lv%d" % j], 16)
+        mm = te.matmul(T.po[:, 0:W], T["v%d" % j][:, :], T["s%d" % j][:, 0:W], start=(i == 0), stop=(i == len(order) - 1))
     mm.then_inc(T.sem.mo, 1)
     ve.wait_ge(T.sem.mo, 1)
     ve.tensor_copy(T.ys[:, 0:W], T.po[:, 0:W]).then_inc(T.sem.cp, 1)

@@ -7,8 +7,6 @@ NH = 6
 SCRATCH = {
     "kd": ("dram", [128, 128], "bfloat16"),
     "vd": ("dram", [128, 128], "bfloat16"),
-    "w0": ("dram", [128, 128], "bfloat16"),
-    "w1": ("dram", [128, 128], "bfloat16"),
     "k0": ("sbuf", [128, 128], "bfloat16"),
     "k1": ("sbuf", [128, 128], "bfloat16"),
     "v0": ("sbuf", [128, 128], "bfloat16"),
@@ -20,10 +18,11 @@ SCRATCH = {
     "ys": ("sbuf", [128, 256], "bfloat16"),
     "p0": ("psum", [128, 512], "float32"),
     "p1": ("psum", [128, 512], "float32"),
-    "po": ("psum", [128, 512], "float32"),
+    "o0": ("psum", [128, 512], "float32"),
+    "o1": ("psum", [128, 512], "float32"),
 }
-SEMAPHORES = ["ldv", "ldk", "lq", "gv", "gk", "sent", "av0", "av1", "ak0", "ak1", "lv0", "lv1",
-              "zf", "m0", "m1", "r0", "r1", "mo", "cp", "st"]
+SEMAPHORES = ["ldv", "ldk", "lq", "gv", "gk", "sent", "av0", "av1", "ak0", "ak1",
+              "zf", "m0", "m1", "r0", "r1", "mo0", "mo1", "cp", "st"]
 
 
 def _count(mask):
@@ -83,8 +82,8 @@ def rank_program(g, core, T, topo):
 
     mine = [j for j, t in enumerate(trees) if t[0] == core]
     for j in mine:
-        g.sync.dma_start(T.vd[:, :], T.v[:, :]).then_inc(T.sem.ldv, 16)
-        g.scalar.dma_start(T.kd[:, :], T.k[:, :]).then_inc(T.sem.ldk, 16)
+        g.sync.dma_start(T.kd[:, :], T.k[:, :]).then_inc(T.sem.ldk, 16)
+        g.scalar.dma_start(T.vd[:, :], T.v[:, :]).then_inc(T.sem.ldv, 16)
 
     if rank is not None:
         W = T.tables["WID"][rank]
@@ -92,27 +91,27 @@ def rank_program(g, core, T, topo):
         g.vector.memset(T.zs[:, 0:W], 0.0).then_inc(T.sem.zf, 1)
         for j in mine:
             g.scalar.dma_start(T["k%d" % j][:, :], T.k[:, :]).then_inc(T.sem["ak%d" % j], 16)
-            g.sync.dma_start(T["v%d" % j][:, :], T.v[:, :]).then_inc(T.sem["lv%d" % j], 16)
+            g.sync.dma_start(T["v%d" % j][:, :], T.v[:, :]).then_inc(T.sem["av%d" % j], 16)
 
     need, late = {}, {}
     for j, (s, direct, helpers, share) in enumerate(trees):
         off = _common(topo, s, direct)
         on = _common(topo, s, helpers) & ~off
-        w, kj, av, ak = "w%d" % j, "k%d" % j, T.sem["av%d" % j], T.sem["ak%d" % j]
+        vj, kj, av, ak = "v%d" % j, "k%d" % j, T.sem["av%d" % j], T.sem["ak%d" % j]
         if core == s:
             need[j], late[j] = 16, (0, 0, 0)
-            g.wait_ge(T.sem.ldv, 16)
-            sent += _send(g, T, topo, core, helpers, "vd", "vd", T.sem.gv, on)
             g.wait_ge(T.sem.ldk, 16)
             sent += _send(g, T, topo, core, helpers, "kd", "kd", T.sem.gk, on)
-            sent += _send(g, T, topo, core, direct, "vd", w, av, off)
+            g.wait_ge(T.sem.ldv, 16)
+            sent += _send(g, T, topo, core, helpers, "vd", "vd", T.sem.gv, on)
             sent += _send(g, T, topo, core, direct, "kd", kj, ak, off)
+            sent += _send(g, T, topo, core, direct, "vd", vj, av, off)
         elif core in share:
             mask = _common(topo, core, share[core])
-            g.wait_ge(T.sem.gv, _count(on))
-            sent += _send(g, T, topo, core, share[core], "vd", w, av, mask)
             g.wait_ge(T.sem.gk, _count(on))
             sent += _send(g, T, topo, core, share[core], "kd", kj, ak, mask)
+            g.wait_ge(T.sem.gv, _count(on))
+            sent += _send(g, T, topo, core, share[core], "vd", vj, av, mask)
         elif core in direct:
             need[j], late[j] = _count(off), (1, direct.index(core), 0)
         elif rank is not None:
@@ -123,12 +122,6 @@ def rank_program(g, core, T, topo):
     if rank is None:
         return
 
-    for j in need:
-        if j not in mine:
-            qu = g.scalar if j % 2 else g.sync
-            qu.wait_ge(T.sem["av%d" % j], need[j])
-            qu.dma_start(T["v%d" % j][:, :], T["w%d" % j][:, :]).then_inc(T.sem["lv%d" % j], 16)
-
     order = sorted(need, key=lambda j: late[j])
     te, ve = g.tensor, g.vector
     te.wait_ge(T.sem.lq, 16)
@@ -138,13 +131,19 @@ def rank_program(g, core, T, topo):
         te.matmul(T["p%d" % j][:, 0:W], T["k%d" % j][:, :], T.qs[:, 0:W], start=True, stop=True).then_inc(T.sem["m%d" % j], 1)
         ve.wait_ge(T.sem["m%d" % j], 1)
         ve.tensor_tensor(T["s%d" % j][:, 0:W], T["p%d" % j][:, 0:W], T.zs[:, 0:W], AluOpType.max).then_inc(T.sem["r%d" % j], 1)
+    H = W // 2 if W >= 128 else W
+    cols = [(0, H), (H, W)] if H < W else [(0, W)]
     for i, j in enumerate(order):
         te.wait_ge(T.sem["r%d" % j], 1)
-        te.wait_ge(T.sem["lv%d" % j], 16)
-        mm = te.matmul(T.po[:, 0:W], T["v%d" % j][:, :], T["s%d" % j][:, 0:W], start=(i == 0), stop=(i == len(order) - 1))
-    mm.then_inc(T.sem.mo, 1)
-    ve.wait_ge(T.sem.mo, 1)
-    ve.tensor_copy(T.ys[:, 0:W], T.po[:, 0:W]).then_inc(T.sem.cp, 1)
-    g.sync.wait_ge(T.sem.cp, 1)
+        te.wait_ge(T.sem["av%d" % j], need[j])
+        for b, (lo, hi) in enumerate(cols):
+            mm = te.matmul(T["o%d" % b][:, 0:hi - lo], T["v%d" % j][:, :], T["s%d" % j][:, lo:hi],
+                           start=(i == 0), stop=(i == len(order) - 1))
+            if i == len(order) - 1:
+                mm.then_inc(T.sem["mo%d" % b], 1)
+    for b, (lo, hi) in enumerate(cols):
+        ve.wait_ge(T.sem["mo%d" % b], 1)
+        ve.tensor_copy(T.ys[:, lo:hi], T["o%d" % b][:, 0:hi - lo]).then_inc(T.sem.cp, 1)
+    g.sync.wait_ge(T.sem.cp, len(cols))
     g.sync.dma_start(T.y[:, 0:W], T.ys[:, 0:W]).then_inc(T.sem.st, 16)
     g.wait_ge(T.sem.st, 16)

from concourse.bass import DstId, RemoteDMATransfer
from concourse.mybir import AluOpType

ND = 3
NH = 6

SCRATCH = {
    "kd": ("dram", [128, 128], "bfloat16"),
    "vd": ("dram", [128, 128], "bfloat16"),
    "k0": ("sbuf", [128, 128], "bfloat16"),
    "k1": ("sbuf", [128, 128], "bfloat16"),
    "v0": ("sbuf", [128, 128], "bfloat16"),
    "v1": ("sbuf", [128, 128], "bfloat16"),
    "qs": ("sbuf", [128, 256], "bfloat16"),
    "zs": ("sbuf", [128, 256], "float32"),
    "s0": ("sbuf", [128, 256], "bfloat16"),
    "s1": ("sbuf", [128, 256], "bfloat16"),
    "ys": ("sbuf", [128, 256], "bfloat16"),
    "p0": ("psum", [128, 512], "float32"),
    "p1": ("psum", [128, 512], "float32"),
    "o0": ("psum", [128, 512], "float32"),
    "o1": ("psum", [128, 512], "float32"),
}
SEMAPHORES = ["ldv", "ldk", "lq", "gv", "gk", "sent", "av0", "av1", "ak0", "ak1",
              "zf", "m0", "m1", "r0", "r1", "mo0", "mo1", "cp", "st"]


def _count(mask):
    return bin(mask).count("1")


def _plan(T, topo):
    cores, wid = list(T.cores), T.tables["WID"]
    world = range(topo.CORES_PER_HOST * (1 + max(topo.host(c) for c in cores)))
    trees = []
    for m in T.tables["MEM"]:
        s = cores[m]
        dests = sorted((c for c in cores if c != s), key=lambda c: -wid[T.rank_of(c)])
        direct = [d for d in dests if topo.may_write(s, d)][:ND]
        todo = [d for d in dests if d not in direct]
        far = [d for d in todo if not topo.may_write(s, d)]
        free = [c for c in world
                if (topo.host(c), topo.chip(c)) == (topo.host(s), topo.chip(s)) and T.rank_of(c) is None]
        owners = [c for c in free if all(topo.may_write(c, d) for d in dests)]
        free = [c for c in free if c in owners or len(far) < len(todo)]
        free.sort(key=lambda c: (c not in owners, topo.die(c) != topo.die(s)))
        free = sorted(free[:NH], key=lambda c: (topo.die(c) != topo.die(s), c not in owners))
        share = {h: [] for h in free}
        while todo:
            for h in free:
                can = [d for d in todo if topo.may_write(h, d)]
                can = [d for d in can if d in far] or can
                if can:
                    share[h].append(can[0])
                    todo.remove(can[0])
        helpers = [h for h in free if share[h]]
        trees.append((s, direct, helpers, {h: share[h] for h in helpers}))
    return trees


def _send(g, T, topo, core, dests, src, out_name, sem, mask):
    ids = []
    for d in dests:
        rid, pid = topo.addr(d, core)
        ids.append(DstId(rid=rid, pnc=pid))
    g.remote_dma_fused([RemoteDMATransfer(dst_ids=ids, dma_engine_mask=mask, remote_sem=sem, srcs=[T[src][:, :]],
                                          dsts=[T[out_name][:, :] for _ in dests], alu_op=0)], local_sem=T.sem.sent)
    return _count(mask)


def _common(topo, core, dests):
    mask = topo.mask(core, dests[0])
    for d in dests:
        mask &= topo.mask(core, d)
    return mask


def rank_program(g, core, T, topo):
    trees = _plan(T, topo)
    rank = T.rank_of(core)
    sent = 0

    mine = [j for j, t in enumerate(trees) if t[0] == core]
    for j in mine:
        g.sync.dma_start(T.kd[:, :], T.k[:, :]).then_inc(T.sem.ldk, 16)
        g.scalar.dma_start(T.vd[:, :], T.v[:, :]).then_inc(T.sem.ldv, 16)

    if rank is not None:
        W = T.tables["WID"][rank]
        g.sync.dma_start(T.qs[:, 0:W], T.q[:, 0:W]).then_inc(T.sem.lq, 16)
        g.vector.memset(T.zs[:, 0:W], 0.0).then_inc(T.sem.zf, 1)
        for j in mine:
            g.scalar.dma_start(T["k%d" % j][:, :], T.k[:, :]).then_inc(T.sem["ak%d" % j], 16)
            g.sync.dma_start(T["v%d" % j][:, :], T.v[:, :]).then_inc(T.sem["av%d" % j], 16)

    need, late = {}, {}
    for j, (s, direct, helpers, share) in enumerate(trees):
        off = _common(topo, s, direct)
        on = _common(topo, s, helpers) & ~off
        vj, kj, av, ak = "v%d" % j, "k%d" % j, T.sem["av%d" % j], T.sem["ak%d" % j]
        if core == s:
            need[j], late[j] = 16, (0, 0, 0)
            g.wait_ge(T.sem.ldk, 16)
            sent += _send(g, T, topo, core, helpers, "kd", "kd", T.sem.gk, on)
            g.wait_ge(T.sem.ldv, 16)
            sent += _send(g, T, topo, core, helpers, "vd", "vd", T.sem.gv, on)
            sent += _send(g, T, topo, core, direct, "kd", kj, ak, off)
            sent += _send(g, T, topo, core, direct, "vd", vj, av, off)
        elif core in share:
            mask = _common(topo, core, share[core])
            g.wait_ge(T.sem.gk, _count(on))
            sent += _send(g, T, topo, core, share[core], "kd", kj, ak, mask)
            g.wait_ge(T.sem.gv, _count(on))
            sent += _send(g, T, topo, core, share[core], "vd", vj, av, mask)
        elif core in direct:
            need[j], late[j] = _count(off), (1, direct.index(core), 0)
        elif rank is not None:
            h = [x for x in helpers if core in share[x]][0]
            need[j], late[j] = _count(_common(topo, h, share[h])), (2, share[h].index(core), helpers.index(h))
    if sent:
        g.wait_ge(T.sem.sent, sent)
    if rank is None:
        return

    order = sorted(need, key=lambda j: late[j])
    te, ve = g.tensor, g.vector
    te.wait_ge(T.sem.lq, 16)
    ve.wait_ge(T.sem.zf, 1)
    for j in order:
        te.wait_ge(T.sem["ak%d" % j], need[j])
        te.matmul(T["p%d" % j][:, 0:W], T["k%d" % j][:, :], T.qs[:, 0:W], start=True, stop=True).then_inc(T.sem["m%d" % j], 1)
        ve.wait_ge(T.sem["m%d" % j], 1)
        ve.tensor_tensor(T["s%d" % j][:, 0:W], T["p%d" % j][:, 0:W], T.zs[:, 0:W], AluOpType.max).then_inc(T.sem["r%d" % j], 1)
    H = W // 2 if W >= 128 else W
    cols = [(0, H), (H, W)] if H < W else [(0, W)]
    for i, j in enumerate(order):
        te.wait_ge(T.sem["r%d" % j], 1)
        te.wait_ge(T.sem["av%d" % j], need[j])
        for b, (lo, hi) in enumerate(cols):
            mm = te.matmul(T["o%d" % b][:, 0:hi - lo], T["v%d" % j][:, :], T["s%d" % j][:, lo:hi],
                           start=(i == 0), stop=(i == len(order) - 1))
            if i == len(order) - 1:
                mm.then_inc(T.sem["mo%d" % b], 1)
    for b, (lo, hi) in enumerate(cols):
        ve.wait_ge(T.sem["mo%d" % b], 1)
        ve.tensor_copy(T.ys[:, lo:hi], T["o%d" % b][:, 0:hi - lo]).then_inc(T.sem.cp, 1)
    g.sync.wait_ge(T.sem.cp, len(cols))
    g.sync.dma_start(T.y[:, 0:W], T.ys[:, 0:W]).then_inc(T.sem.st, 16)
    g.wait_ge(T.sem.st, 16)
